import numpy as np
import ml_dtypes


def mxq(x, axis, fmt="e4m3"):
    dtype, down = {"e4m3": (ml_dtypes.float8_e4m3fn, 7), "e5m2": (ml_dtypes.float8_e5m2, 14)}[fmt]
    v = np.moveaxis(np.asarray(x, np.float32).astype(ml_dtypes.bfloat16).astype(np.float64), axis, -1)
    blocks = v.reshape(v.shape[:-1] + (-1, 32))
    amax = np.abs(blocks).max(-1, keepdims=True)
    byte = np.maximum(np.where(amax > 0, np.frexp(amax)[1] - 1 + 127, 0) - down, 1)
    scale = np.exp2(byte - 127.0)
    codes = (blocks / scale).astype(np.float32).astype(dtype).astype(np.float64)
    return np.moveaxis((codes * scale).reshape(v.shape), -1, axis)


WIDE = False


def mx_kscale(k):
    if not WIDE:
        return np.ones(k)
    levels = np.array([30, -30])
    if k % 512:
        return np.exp2(np.random.permutation(np.resize(levels, k // 32))).repeat(32)
    a = np.empty((k // 512, 16))
    for p in range(k // 512):
        a[p, :8] = np.random.permutation(np.resize(levels, 8))
        for g in range(8):
            far = levels[np.abs(levels - a[p, g]) >= 10]
            a[p, g + 8] = far[np.random.randint(len(far))]
    return np.exp2(a.ravel()).repeat(32)


BF16 = ml_dtypes.bfloat16


def bf(x):
    return np.asarray(x, np.float32).astype(BF16)


def f64(x):
    return np.asarray(x).astype(np.float64)


E2M1 = np.array([0.0, 0.5, 1.0, 1.5, 2.0, 3.0, 4.0, 6.0, -0.0, -0.5, -1.0, -1.5, -2.0, -3.0, -4.0, -6.0])


def pack_weight(w, fmt):
    k, n = w.shape
    w = f64(bf(w)).reshape(k // 32, 32, n)
    amax = np.abs(w).max(1)
    if fmt in ("e4m3", "e5m2"):
        byte = np.frexp(amax)[1] - 1 + 127 - (7 if fmt == "e4m3" else 14)
    else:
        mant, ex = np.frexp(amax / 6.0)
        byte = np.where(mant > 0.5, ex, ex - 1) + 127
    byte = np.clip(np.where(amax > 0, byte, 1), 1, 254)
    scaled = (w * np.exp2(127.0 - byte)[:, None, :]).reshape(k, n).astype(np.float32)
    by_word = np.ascontiguousarray(scaled.reshape(k // 512, 128, 4, n).transpose(0, 1, 3, 2))
    if fmt in ("e4m3", "e5m2"):
        words = by_word.astype(ml_dtypes.float8_e4m3fn if fmt == "e4m3" else ml_dtypes.float8_e5m2).view(np.uint8)
    else:
        c = by_word.astype(ml_dtypes.float4_e2m1fn).view(np.uint8) & 0xF
        words = c[..., 0::2] | (c[..., 1::2] << 4)
    return np.ascontiguousarray(words), np.ascontiguousarray(byte.astype(np.uint8).reshape(k // 512, 16, n))


def unpack_weight(words, scales, fmt):
    g, p, n, _ = words.shape
    if fmt in ("e4m3", "e5m2"):
        vals = np.ascontiguousarray(words).view(ml_dtypes.float8_e4m3fn if fmt == "e4m3" else ml_dtypes.float8_e5m2).astype(np.float64)
    else:
        nib = np.empty((g, p, n, 4), np.uint8)
        nib[..., 0::2] = words & 0xF
        nib[..., 1::2] = words >> 4
        vals = E2M1[nib]
    vals = vals * np.repeat(np.exp2(scales.astype(np.float64) - 127.0), 8, axis=1)[..., None]
    return vals.transpose(0, 1, 3, 2).reshape(g * 512, n)


T, D, F = 4096, 512, 2048


def setup_inputs():
    s = mx_kscale(T)
    x = np.random.standard_normal((T, D)) * s[:, None]
    size = np.exp(0.5 * np.random.standard_normal((T, 1)))
    G = np.random.standard_normal((T, F)) * size / np.sqrt(T) / s[:, None]
    g_words, g_scales = pack_weight(G, "e5m2")
    return {"x": bf(x),
            "g_words": g_words,
            "g_scales": g_scales,
            "gain": bf(1 + 0.1 * np.random.standard_normal(D)),
            "w": bf(np.random.standard_normal((D, F)) / np.sqrt(D))}


def reference(x, g_words, g_scales, gain, w):
    G = unpack_weight(g_words, g_scales, "e5m2")
    xq = mxq(f64(x), 0, "e4m3")
    a = xq.T @ G
    dw = f64(gain)[:, None] * a
    dgain = (f64(w) * a).sum(axis=1)
    return dw, dgain

@@ -1,0 +1,222 @@
+from contextlib import ExitStack
+
+import concourse.mybir as mybir
+from concourse.masks import make_identity
+
+T, D, F = 4096, 512, 2048
+FLOPS = 2 * T * D * F
+
+F32 = mybir.dt.float32
+BF16 = mybir.dt.bfloat16
+I32 = mybir.dt.int32
+U32 = mybir.dt.uint32
+U8 = mybir.dt.uint8
+E4X4 = mybir.dt.float8_e4m3fn_x4
+E5X4 = mybir.dt.float8_e5m2_x4
+MULT = mybir.AluOpType.mult
+ADD = mybir.AluOpType.add
+COPY = mybir.ActivationFunctionType.Copy
+AXIS_X = mybir.AxisListType.X
+
+P = 128
+PACK = 4
+GROUPS = T // (P * PACK)
+M_TILES = D // P
+N = 512
+HALF = 1024
+
+
+def tile_up_projection_gain_grads_e2_kernel(tc, x, g_words, g_scales, gain, w, out_0, out_1):
+    nc = tc.nc
+    x_rows = x.rearrange("(g p j) d -> g p j d", p=P, j=PACK)
+    words = g_words.rearrange("g p n t -> g p (n t)")
+    scale_rows = g_scales.bitcast(I32).rearrange("g (q r) n -> r q g n", r=4)
+    w_rows = w.rearrange("(m p) n -> p m n", p=P)
+    dw_rows = out_0.rearrange("(m p) n -> m p n", p=P)
+
+    with ExitStack() as ctx:
+        keep = ctx.enter_context(tc.tile_pool(name="keep", bufs=1))
+        grp = ctx.enter_context(tc.tile_pool(name="grp", bufs=3))
+        junkp = ctx.enter_context(tc.tile_pool(name="junkp", bufs=2))
+        psum = ctx.enter_context(tc.psum_pool(name="psum", bufs=1))
+        ctx.enter_context(tc.manual_schedule())
+
+        x_raw = [keep.tile([P, PACK, D], BF16, name=f"x_raw{g}", align_bytes=64) for g in range(GROUPS)]
+        x_codes = keep.tile([P, GROUPS, D], U32, name="x_codes", align_bytes=64)
+        x_scales = keep.tile([P, GROUPS, D], U8, name="x_scales", align_bytes=64)
+        g_codes = [
+            [keep.tile([P, HALF], U32, name=f"g_codes{h}_{g}", align_bytes=64) for g in range(GROUPS)] for h in range(2)
+        ]
+        g_planes = [keep.tile([P, GROUPS, HALF], U8, name=f"g_planes{h}", align_bytes=64) for h in range(2)]
+        w_sb = keep.tile([P, M_TILES, F], BF16, name="w_sb", align_bytes=64)
+        a_raw = [keep.tile([P, HALF], F32, name=f"a_raw{m}", align_bytes=64) for m in range(M_TILES)]
+        dw_sb = [
+            [keep.tile([P, HALF], F32, name=f"dw_sb{h}_{m}", align_bytes=64) for m in range(M_TILES)] for h in range(2)
+        ]
+        gain_rows = keep.tile([P, P], BF16, name="gain_rows", align_bytes=64)
+        gain_col = keep.tile([P, M_TILES], F32, name="gain_col", align_bytes=64)
+        ident = keep.tile([P, P], F32, name="ident", align_bytes=64)
+        ident_bf = keep.tile([P, P], BF16, name="ident_bf", align_bytes=64)
+        early = keep.tile([P, P], F32, name="early", align_bytes=64)
+        late = keep.tile([P, P], F32, name="late", align_bytes=64)
+        parts = keep.tile([P, M_TILES, 4], F32, name="parts", align_bytes=64)
+        dgain_sb = keep.tile([M_TILES, P], F32, name="dgain_sb", align_bytes=64)
+
+        def bank(b, what):
+            return psum.tile([P, N], F32, name=what, tag=f"bank{b}")
+
+        def zero_planes(h, g0, g1):
+            nc.vector.memset(g_planes[h][:, g0:g1, :].rearrange("p g n -> p (g n)").bitcast(I32), 0)
+
+        def load_scales(h, g0, g1):
+            for r in range(4):
+                nc.sync.dma_start(
+                    out=g_planes[h][r:P:32, g0:g1, :].bitcast(I32),
+                    in_=scale_rows[r, :, g0:g1, h * (HALF // 4) : (h + 1) * (HALF // 4)],
+                )
+
+        def load_x(g):
+            nc.sync.dma_start(out=x_raw[g][:], in_=x_rows[g])
+
+        def load_g(h, g):
+            nc.sync.dma_start(
+                out=g_codes[h][g][:].bitcast(I32),
+                in_=words[g, :, h * HALF * 4 : (h + 1) * HALF * 4].bitcast(I32),
+            )
+
+        def load_w(m0, m1):
+            nc.sync.dma_start(out=w_sb[:, m0:m1, :], in_=w_rows[:, m0:m1, :])
+
+        zero_planes(0, 0, 2)
+        nc.gpsimd.memset(gain_rows[:], 0.0)
+        nc.scalar.dma_start(out=gain_rows[0:M_TILES, :], in_=gain.rearrange("(m d) -> m d", m=M_TILES))
+        make_identity(nc, ident[:])
+        nc.gpsimd.memset(early[:], 0.0)
+        nc.gpsimd.memset(late[:], 0.0)
+        zero_planes(0, 2, GROUPS)
+        zero_planes(1, 0, GROUPS)
+
+        load_scales(0, 0, 2)
+        for g in range(GROUPS):
+            load_x(g)
+            load_g(0, g)
+            if g == 1:
+                load_scales(0, 2, GROUPS)
+        load_scales(1, 0, GROUPS)
+        for g in range(GROUPS):
+            load_g(1, g)
+            if g == 3:
+                load_w(0, 2)
+        load_w(2, 4)
+
+        nc.vector.tensor_copy(out=ident_bf[:], in_=ident[:])
+
+        gain_ps = bank(7, "gain_ps")
+        nc.tensor.matmul(gain_ps[:, 0:M_TILES], lhsT=gain_rows[:], rhs=ident_bf[:, 0:M_TILES], start=True, stop=True)
+        nc.vector.tensor_copy(out=gain_col[:], in_=gain_ps[:, 0:M_TILES])
+
+        def quantise(g):
+            lay = grp.tile([P, D, PACK], BF16, name="lay", align_bytes=64)
+            src = x_raw[g][:].rearrange("p j d -> p d j")
+            for a in (0, 128):
+                nc.vector.tensor_copy(out=lay[:, a : a + 128, :], in_=src[:, a : a + 128, :])
+            for a in (256, 384):
+                nc.scalar.copy(lay[:, a : a + 128, :], src[:, a : a + 128, :])
+            for a, b in ((0, 128), (128, 256), (256, 512)):
+                nc.vector.quantize_mx(
+                    out=x_codes[:, g, a:b].bitcast(E4X4),
+                    scales=x_scales[:, g, a:b],
+                    in_=lay[:, a:b, :].rearrange("p d j -> p (d j)"),
+                )
+
+        def mx_pass(acc, h, g, m, n):
+            nc.tensor.matmul_mx(
+                out=acc[:],
+                lhsT=x_codes[:, g, m * P : (m + 1) * P].bitcast(E4X4),
+                lhsT_scale=x_scales[:, g, m * P : (m + 1) * P],
+                rhs=g_codes[h][g][:, n * N : (n + 1) * N].bitcast(E5X4),
+                rhs_scale=g_planes[h][:, g, n * N : (n + 1) * N],
+                start=(g == 0),
+                stop=(g == GROUPS - 1),
+            )
+
+        acc = [[bank(4 * n + m, f"acc0_{n}_{m}") for m in range(M_TILES)] for n in range(2)]
+        for g in range(GROUPS):
+            quantise(g)
+            if g < GROUPS - 2:
+                for m in range(M_TILES):
+                    for n in range(2):
+                        mx_pass(acc[n][m], 0, g, m, n)
+        for n in range(2):
+            for g in (GROUPS - 2, GROUPS - 1):
+                for m in range(M_TILES):
+                    mx_pass(acc[n][m], 0, g, m, n)
+        for n in range(2):
+            for m in range(M_TILES):
+                nc.scalar.copy(a_raw[m][:, n * N : (n + 1) * N], acc[n][m][:])
+
+        acc2 = [[bank(2 * m + n, f"acc1_{n}_{m}") for n in range(2)] for m in range(2)]
+        for g in range(GROUPS):
+            for m in range(2):
+                for n in range(2):
+                    mx_pass(acc2[m][n], 1, g, m, n)
+
+        for m in range(M_TILES):
+            nc.vector.tensor_scalar(
+                out=dw_sb[0][m][:], in0=a_raw[m][:], scalar1=gain_col[:, m : m + 1], scalar2=None, op0=MULT
+            )
+            nc.sync.dma_start(out=dw_rows[m, :, 0:HALF], in_=dw_sb[0][m][:])
+
+        def weigh_sweep1(m):
+            junk = junkp.tile([P, HALF], F32, name="junk")
+            nc.vector.scalar_tensor_tensor(
+                out=junk[:], in0=a_raw[m][:], scalar=1.0, in1=w_sb[:, m, 0:HALF], op0=MULT, op1=MULT,
+                accum_out=parts[:, m, 0:1],
+            )
+
+        def weigh_bank(a, m, n, into):
+            junk = junkp.tile([P, HALF], F32, name="junk")
+            nc.vector.scalar_tensor_tensor(
+                out=junk[:, 0:N], in0=a[:], scalar=1.0, in1=w_sb[:, m, HALF + n * N : HALF + (n + 1) * N],
+                op0=MULT, op1=MULT, accum_out=into,
+            )
+
+        def scale_bank(a, m, n):
+            nc.scalar.activation(
+                out=dw_sb[1][m][:, n * N : (n + 1) * N], in_=a[:], func=COPY, scale=gain_col[:, m : m + 1]
+            )
+
+        weigh_sweep1(0)
+        weigh_sweep1(1)
+        for m in range(2):
+            for n in range(2):
+                scale_bank(acc2[m][n], m, n)
+                weigh_bank(acc2[m][n], m, n, parts[:, m, 1 + n : 2 + n])
+            nc.sync.dma_start(out=dw_rows[m, :, HALF:F], in_=dw_sb[1][m][:])
+        weigh_sweep1(2)
+        weigh_sweep1(3)
+
+        acc3 = {}
+        for m in (2, 3):
+            for n in range(2):
+                acc3[m, n] = bank(2 * m + n, f"acc2_{n}_{m}")
+                for g in range(GROUPS):
+                    mx_pass(acc3[m, n], 1, g, m, n)
+        scale_bank(acc3[2, 0], 2, 0)
+        weigh_bank(acc3[2, 0], 2, 0, parts[:, 2, 1:2])
+        scale_bank(acc3[2, 1], 2, 1)
+        weigh_bank(acc3[2, 1], 2, 1, parts[:, 2, 2:3])
+        nc.sync.dma_start(out=dw_rows[2, :, HALF:F], in_=dw_sb[1][2][:])
+        scale_bank(acc3[3, 0], 3, 0)
+        weigh_bank(acc3[3, 0], 3, 0, parts[:, 3, 1:2])
+        nc.sync.dma_start(out=dw_rows[3, :, HALF : HALF + N], in_=dw_sb[1][3][:, 0:N])
+        nc.vector.tensor_reduce(out=early[:, 0:3], in_=parts[:, 0:3, 0:3], axis=AXIS_X, op=ADD)
+        nc.vector.tensor_reduce(out=early[:, 3:4], in_=parts[:, 3:4, 0:2], axis=AXIS_X, op=ADD)
+        dg = bank(0, "dg")
+        nc.tensor.matmul(dg[:, 0:P], lhsT=early[:], rhs=ident[:], start=True, stop=False)
+        weigh_bank(acc3[3, 1], 3, 1, late[:, 3:4])
+        scale_bank(acc3[3, 1], 3, 1)
+        nc.sync.dma_start(out=dw_rows[3, :, HALF + N : F], in_=dw_sb[1][3][:, N:HALF])
+        nc.tensor.matmul(dg[:, 0:P], lhsT=late[:], rhs=ident[:], start=False, stop=True)
+        nc.scalar.copy(dgain_sb[:], dg[0:M_TILES, 0:P])
+        nc.sync.dma_start(out=out_1.rearrange("(m d) -> m d", m=M_TILES), in_=dgain_sb[:])

@@ -70,7 +70,7 @@ def tile_up_projection_gain_grads_e2_kernel(tc, x, g_words, g_scales, gain, w, o
 
         def load_scales(h, g0, g1):
             for r in range(4):
-                nc.sync.dma_start(
+                nc.gpsimd.dma_start(
                     out=g_planes[h][r:P:32, g0:g1, :].bitcast(I32),
                     in_=scale_rows[r, :, g0:g1, h * (HALF // 4) : (h + 1) * (HALF // 4)],
                 )
@@ -90,22 +90,21 @@ def tile_up_projection_gain_grads_e2_kernel(tc, x, g_words, g_scales, gain, w, o
         zero_planes(0, 0, 2)
         nc.gpsimd.memset(gain_rows[:], 0.0)
         nc.scalar.dma_start(out=gain_rows[0:M_TILES, :], in_=gain.rearrange("(m d) -> m d", m=M_TILES))
-        make_identity(nc, ident[:])
-        nc.gpsimd.memset(early[:], 0.0)
-        nc.gpsimd.memset(late[:], 0.0)
         zero_planes(0, 2, GROUPS)
         zero_planes(1, 0, GROUPS)
 
         load_scales(0, 0, 2)
+        make_identity(nc, ident[:])
+        load_scales(0, 2, GROUPS)
+        load_scales(1, 0, GROUPS)
+        nc.gpsimd.memset(early[:], 0.0)
+        nc.gpsimd.memset(late[:], 0.0)
         for g in range(GROUPS):
             load_x(g)
             load_g(0, g)
-            if g == 1:
-                load_scales(0, 2, GROUPS)
-        load_scales(1, 0, GROUPS)
         for g in range(GROUPS):
             load_g(1, g)
-            if g == 3:
+            if g == 5:
                 load_w(0, 2)
         load_w(2, 4)
 

@@ -24,15 +24,16 @@ GROUPS = T // (P * PACK)
 M_TILES = D // P
 N = 512
 HALF = 1024
+SCALE_BATCHES = ((0, 0, 2), (0, 2, GROUPS), (1, 0, GROUPS))
 
 
 def tile_up_projection_gain_grads_e2_kernel(tc, x, g_words, g_scales, gain, w, out_0, out_1):
     nc = tc.nc
-    x_rows = x.rearrange("(g p j) d -> g p j d", p=P, j=PACK)
-    words = g_words.rearrange("g p n t -> g p (n t)")
+    x_rows = x.rearrange("(g p j) d -> p g (j d)", p=P, j=PACK)
+    words = g_words.rearrange("g p n t -> p g (n t)")
     scale_rows = g_scales.bitcast(I32).rearrange("g (q r) n -> r q g n", r=4)
     w_rows = w.rearrange("(m p) n -> p m n", p=P)
-    dw_rows = out_0.rearrange("(m p) n -> m p n", p=P)
+    dw_rows = out_0.rearrange("(m p) n -> p m n", p=P)
 
     with ExitStack() as ctx:
         keep = ctx.enter_context(tc.tile_pool(name="keep", bufs=1))
@@ -41,18 +42,23 @@ def tile_up_projection_gain_grads_e2_kernel(tc, x, g_words, g_scales, gain, w, o
         psum = ctx.enter_context(tc.psum_pool(name="psum", bufs=1))
         ctx.enter_context(tc.manual_schedule())
 
-        x_raw = [keep.tile([P, PACK, D], BF16, name=f"x_raw{g}", align_bytes=64) for g in range(GROUPS)]
+        x_raw = keep.tile([P, GROUPS, PACK, D], BF16, name="x_raw", align_bytes=64)
         x_codes = keep.tile([P, GROUPS, D], U32, name="x_codes", align_bytes=64)
         x_scales = keep.tile([P, GROUPS, D], U8, name="x_scales", align_bytes=64)
-        g_codes = [
-            [keep.tile([P, HALF], U32, name=f"g_codes{h}_{g}", align_bytes=64) for g in range(GROUPS)] for h in range(2)
-        ]
-        g_planes = [keep.tile([P, GROUPS, HALF], U8, name=f"g_planes{h}", align_bytes=64) for h in range(2)]
+        g_codes = [keep.tile([P, GROUPS, HALF], U32, name=f"g_codes{h}", align_bytes=64) for h in range(2)]
+        g_planes = {
+            (h, g0, g1): keep.tile([P, g1 - g0, HALF], U8, name=f"g_planes{h}_{g0}", align_bytes=64)
+            for h, g0, g1 in SCALE_BATCHES
+        }
+
+        def plane(h, g):
+            for hh, g0, g1 in SCALE_BATCHES:
+                if hh == h and g0 <= g < g1:
+                    return g_planes[hh, g0, g1][:, g - g0, :]
+            raise ValueError("no scale tile for this group")
         w_sb = keep.tile([P, M_TILES, F], BF16, name="w_sb", align_bytes=64)
-        a_raw = [keep.tile([P, HALF], F32, name=f"a_raw{m}", align_bytes=64) for m in range(M_TILES)]
-        dw_sb = [
-            [keep.tile([P, HALF], F32, name=f"dw_sb{h}_{m}", align_bytes=64) for m in range(M_TILES)] for h in range(2)
-        ]
+        a_raw = keep.tile([P, M_TILES, HALF], F32, name="a_raw", align_bytes=64)
+        dw_sb = [keep.tile([P, M_TILES, HALF], F32, name=f"dw_sb{h}", align_bytes=64) for h in range(2)]
         gain_rows = keep.tile([P, P], BF16, name="gain_rows", align_bytes=64)
         gain_col = keep.tile([P, M_TILES], F32, name="gain_col", align_bytes=64)
         ident = keep.tile([P, P], F32, name="ident", align_bytes=64)
@@ -66,57 +72,62 @@ def tile_up_projection_gain_grads_e2_kernel(tc, x, g_words, g_scales, gain, w, o
             return psum.tile([P, N], F32, name=what, tag=f"bank{b}")
 
         def zero_planes(h, g0, g1):
-            nc.vector.memset(g_planes[h][:, g0:g1, :].rearrange("p g n -> p (g n)").bitcast(I32), 0)
+            nc.vector.memset(g_planes[h, g0, g1][:].rearrange("p g n -> p (g n)").bitcast(I32), 0)
 
         def load_scales(h, g0, g1):
             for r in range(4):
-                nc.gpsimd.dma_start(
-                    out=g_planes[h][r:P:32, g0:g1, :].bitcast(I32),
+                nc.sync.dma_start(
+                    out=g_planes[h, g0, g1][r:P:32].bitcast(I32),
                     in_=scale_rows[r, :, g0:g1, h * (HALF // 4) : (h + 1) * (HALF // 4)],
                 )
 
-        def load_x(g):
-            nc.sync.dma_start(out=x_raw[g][:], in_=x_rows[g])
+        def load_x(g0, g1):
+            nc.sync.dma_start(out=x_raw[:, g0:g1].rearrange("p g j d -> p g (j d)"), in_=x_rows[:, g0:g1, :])
 
-        def load_g(h, g):
+        def load_g(h, g0, g1):
             nc.sync.dma_start(
-                out=g_codes[h][g][:].bitcast(I32),
-                in_=words[g, :, h * HALF * 4 : (h + 1) * HALF * 4].bitcast(I32),
+                out=g_codes[h][:, g0:g1, :].bitcast(I32),
+                in_=words[:, g0:g1, h * HALF * 4 : (h + 1) * HALF * 4].bitcast(I32),
             )
 
         def load_w(m0, m1):
             nc.sync.dma_start(out=w_sb[:, m0:m1, :], in_=w_rows[:, m0:m1, :])
 
+        def store(h, m0, m1, n0, n1):
+            nc.sync.dma_start(out=dw_rows[:, m0:m1, h * HALF + n0 : h * HALF + n1], in_=dw_sb[h][:, m0:m1, n0:n1])
+
         zero_planes(0, 0, 2)
         nc.gpsimd.memset(gain_rows[:], 0.0)
-        nc.scalar.dma_start(out=gain_rows[0:M_TILES, :], in_=gain.rearrange("(m d) -> m d", m=M_TILES))
+        make_identity(nc, ident[:])
+        nc.gpsimd.memset(early[:], 0.0)
+        nc.gpsimd.memset(late[:], 0.0)
         zero_planes(0, 2, GROUPS)
         zero_planes(1, 0, GROUPS)
 
-        load_scales(0, 0, 2)
-        make_identity(nc, ident[:])
-        load_scales(0, 2, GROUPS)
+        for g in range(GROUPS):
+            load_x(g, g + 1)
+            if g == 0:
+                nc.sync.dma_start(out=gain_rows[0:M_TILES, :], in_=gain.rearrange("(m d) -> m d", m=M_TILES))
+                load_scales(0, 0, 2)
+            load_g(0, g, g + 1)
+            if g == 1:
+                load_scales(0, 2, GROUPS)
         load_scales(1, 0, GROUPS)
-        nc.gpsimd.memset(early[:], 0.0)
-        nc.gpsimd.memset(late[:], 0.0)
         for g in range(GROUPS):
-            load_x(g)
-            load_g(0, g)
-        for g in range(GROUPS):
-            load_g(1, g)
-            if g == 5:
-                load_w(0, 2)
-        load_w(2, 4)
+            load_g(1, g, g + 1)
+            if g == 3:
+                load_w(0, 1)
+        for m in range(1, M_TILES):
+            load_w(m, m + 1)
 
         nc.vector.tensor_copy(out=ident_bf[:], in_=ident[:])
 
         gain_ps = bank(7, "gain_ps")
         nc.tensor.matmul(gain_ps[:, 0:M_TILES], lhsT=gain_rows[:], rhs=ident_bf[:, 0:M_TILES], start=True, stop=True)
-        nc.vector.tensor_copy(out=gain_col[:], in_=gain_ps[:, 0:M_TILES])
 
         def quantise(g):
             lay = grp.tile([P, D, PACK], BF16, name="lay", align_bytes=64)
-            src = x_raw[g][:].rearrange("p j d -> p d j")
+            src = x_raw[:, g].rearrange("p j d -> p d j")
             for a in (0, 128):
                 nc.vector.tensor_copy(out=lay[:, a : a + 128, :], in_=src[:, a : a + 128, :])
             for a in (256, 384):
@@ -133,8 +144,8 @@ def tile_up_projection_gain_grads_e2_kernel(tc, x, g_words, g_scales, gain, w, o
                 out=acc[:],
                 lhsT=x_codes[:, g, m * P : (m + 1) * P].bitcast(E4X4),
                 lhsT_scale=x_scales[:, g, m * P : (m + 1) * P],
-                rhs=g_codes[h][g][:, n * N : (n + 1) * N].bitcast(E5X4),
-                rhs_scale=g_planes[h][:, g, n * N : (n + 1) * N],
+                rhs=g_codes[h][:, g, n * N : (n + 1) * N].bitcast(E5X4),
+                rhs_scale=plane(h, g)[:, n * N : (n + 1) * N],
                 start=(g == 0),
                 stop=(g == GROUPS - 1),
             )
@@ -142,80 +153,75 @@ def tile_up_projection_gain_grads_e2_kernel(tc, x, g_words, g_scales, gain, w, o
         acc = [[bank(4 * n + m, f"acc0_{n}_{m}") for m in range(M_TILES)] for n in range(2)]
         for g in range(GROUPS):
             quantise(g)
-            if g < GROUPS - 2:
+            if g == 0:
+                nc.vector.tensor_copy(out=gain_col[:], in_=gain_ps[:, 0:M_TILES])
+            if g < GROUPS - 1:
                 for m in range(M_TILES):
                     for n in range(2):
                         mx_pass(acc[n][m], 0, g, m, n)
         for n in range(2):
-            for g in (GROUPS - 2, GROUPS - 1):
-                for m in range(M_TILES):
-                    mx_pass(acc[n][m], 0, g, m, n)
+            for m in range(M_TILES):
+                mx_pass(acc[n][m], 0, GROUPS - 1, m, n)
         for n in range(2):
             for m in range(M_TILES):
-                nc.scalar.copy(a_raw[m][:, n * N : (n + 1) * N], acc[n][m][:])
+                half = a_raw[:, m, n * N : (n + 1) * N]
+                if m % 2 == 0:
+                    nc.scalar.copy(half, acc[n][m][:])
+                else:
+                    nc.vector.tensor_copy(out=half, in_=acc[n][m][:])
 
-        acc2 = [[bank(2 * m + n, f"acc1_{n}_{m}") for n in range(2)] for m in range(2)]
-        for g in range(GROUPS):
-            for m in range(2):
+        acc2 = [[bank(2 * m + n, f"acc1_{n}_{m}") for n in range(2)] for m in range(M_TILES)]
+        for g in range(GROUPS // 2):
+            for m in range(M_TILES):
                 for n in range(2):
+                    mx_pass(acc2[m][n], 1, g, m, n)
+        for m in range(M_TILES):
+            for n in range(2):
+                for g in range(GROUPS // 2, GROUPS):
                     mx_pass(acc2[m][n], 1, g, m, n)
 
         for m in range(M_TILES):
-            nc.vector.tensor_scalar(
-                out=dw_sb[0][m][:], in0=a_raw[m][:], scalar1=gain_col[:, m : m + 1], scalar2=None, op0=MULT
-            )
-            nc.sync.dma_start(out=dw_rows[m, :, 0:HALF], in_=dw_sb[0][m][:])
+            nc.scalar.activation(out=dw_sb[0][:, m, :], in_=a_raw[:, m, :], func=COPY, scale=gain_col[:, m : m + 1])
+        store(0, 0, 2, 0, HALF)
+        store(0, 2, 4, 0, HALF)
 
         def weigh_sweep1(m):
             junk = junkp.tile([P, HALF], F32, name="junk")
             nc.vector.scalar_tensor_tensor(
-                out=junk[:], in0=a_raw[m][:], scalar=1.0, in1=w_sb[:, m, 0:HALF], op0=MULT, op1=MULT,
+                out=junk[:], in0=a_raw[:, m, :], scalar=1.0, in1=w_sb[:, m, 0:HALF], op0=MULT, op1=MULT,
                 accum_out=parts[:, m, 0:1],
             )
 
-        def weigh_bank(a, m, n, into):
+        def weigh_bank(m, n, into):
             junk = junkp.tile([P, HALF], F32, name="junk")
             nc.vector.scalar_tensor_tensor(
-                out=junk[:, 0:N], in0=a[:], scalar=1.0, in1=w_sb[:, m, HALF + n * N : HALF + (n + 1) * N],
+                out=junk[:, 0:N], in0=acc2[m][n][:], scalar=1.0, in1=w_sb[:, m, HALF + n * N : HALF + (n + 1) * N],
                 op0=MULT, op1=MULT, accum_out=into,
             )
 
-        def scale_bank(a, m, n):
+        def scale_bank(m, n):
             nc.scalar.activation(
-                out=dw_sb[1][m][:, n * N : (n + 1) * N], in_=a[:], func=COPY, scale=gain_col[:, m : m + 1]
+                out=dw_sb[1][:, m, n * N : (n + 1) * N], in_=acc2[m][n][:], func=COPY, scale=gain_col[:, m : m + 1]
             )
 
         weigh_sweep1(0)
-        weigh_sweep1(1)
-        for m in range(2):
+        for m in range(M_TILES - 1):
+            weigh_sweep1(m + 1)
             for n in range(2):
-                scale_bank(acc2[m][n], m, n)
-                weigh_bank(acc2[m][n], m, n, parts[:, m, 1 + n : 2 + n])
-            nc.sync.dma_start(out=dw_rows[m, :, HALF:F], in_=dw_sb[1][m][:])
-        weigh_sweep1(2)
-        weigh_sweep1(3)
-
-        acc3 = {}
-        for m in (2, 3):
-            for n in range(2):
-                acc3[m, n] = bank(2 * m + n, f"acc2_{n}_{m}")
-                for g in range(GROUPS):
-                    mx_pass(acc3[m, n], 1, g, m, n)
-        scale_bank(acc3[2, 0], 2, 0)
-        weigh_bank(acc3[2, 0], 2, 0, parts[:, 2, 1:2])
-        scale_bank(acc3[2, 1], 2, 1)
-        weigh_bank(acc3[2, 1], 2, 1, parts[:, 2, 2:3])
-        nc.sync.dma_start(out=dw_rows[2, :, HALF:F], in_=dw_sb[1][2][:])
-        scale_bank(acc3[3, 0], 3, 0)
-        weigh_bank(acc3[3, 0], 3, 0, parts[:, 3, 1:2])
-        nc.sync.dma_start(out=dw_rows[3, :, HALF : HALF + N], in_=dw_sb[1][3][:, 0:N])
-        nc.vector.tensor_reduce(out=early[:, 0:3], in_=parts[:, 0:3, 0:3], axis=AXIS_X, op=ADD)
-        nc.vector.tensor_reduce(out=early[:, 3:4], in_=parts[:, 3:4, 0:2], axis=AXIS_X, op=ADD)
+                scale_bank(m, n)
+                weigh_bank(m, n, parts[:, m, 1 + n : 2 + n])
+            store(1, m, m + 1, 0, HALF)
+        m = M_TILES - 1
+        scale_bank(m, 0)
+        weigh_bank(m, 0, parts[:, m, 1:2])
+        store(1, m, m + 1, 0, N)
+        nc.vector.tensor_reduce(out=early[:, 0:m], in_=parts[:, 0:m, 0:3], axis=AXIS_X, op=ADD)
+        nc.vector.tensor_reduce(out=early[:, m : m + 1], in_=parts[:, m : m + 1, 0:2], axis=AXIS_X, op=ADD)
         dg = bank(0, "dg")
         nc.tensor.matmul(dg[:, 0:P], lhsT=early[:], rhs=ident[:], start=True, stop=False)
-        weigh_bank(acc3[3, 1], 3, 1, late[:, 3:4])
-        scale_bank(acc3[3, 1], 3, 1)
-        nc.sync.dma_start(out=dw_rows[3, :, HALF + N : F], in_=dw_sb[1][3][:, N:HALF])
+        weigh_bank(m, 1, late[:, m : m + 1])
+        scale_bank(m, 1)
+        store(1, m, m + 1, N, HALF)
         nc.tensor.matmul(dg[:, 0:P], lhsT=late[:], rhs=ident[:], start=False, stop=True)
         nc.scalar.copy(dgain_sb[:], dg[0:M_TILES, 0:P])
         nc.sync.dma_start(out=out_1.rearrange("(m d) -> m d", m=M_TILES), in_=dgain_sb[:])

@@ -24,7 +24,7 @@ GROUPS = T // (P * PACK)
 M_TILES = D // P
 N = 512
 HALF = 1024
-SCALE_BATCHES = ((0, 0, 2), (0, 2, GROUPS), (1, 0, GROUPS))
+SCALE_BATCHES = ((0, 0, 2), (0, 2, 4), (0, 4, GROUPS), (1, 0, GROUPS))
 
 
 def tile_up_projection_gain_grads_e2_kernel(tc, x, g_words, g_scales, gain, w, out_0, out_1):
@@ -74,9 +74,9 @@ def tile_up_projection_gain_grads_e2_kernel(tc, x, g_words, g_scales, gain, w, o
         def zero_planes(h, g0, g1):
             nc.vector.memset(g_planes[h, g0, g1][:].rearrange("p g n -> p (g n)").bitcast(I32), 0)
 
-        def load_scales(h, g0, g1):
+        def load_scales(queue, h, g0, g1):
             for r in range(4):
-                nc.sync.dma_start(
+                queue.dma_start(
                     out=g_planes[h, g0, g1][r:P:32].bitcast(I32),
                     in_=scale_rows[r, :, g0:g1, h * (HALF // 4) : (h + 1) * (HALF // 4)],
                 )
@@ -93,32 +93,36 @@ def tile_up_projection_gain_grads_e2_kernel(tc, x, g_words, g_scales, gain, w, o
         def load_w(m0, m1):
             nc.sync.dma_start(out=w_sb[:, m0:m1, :], in_=w_rows[:, m0:m1, :])
 
-        def store(h, m0, m1, n0, n1):
-            nc.sync.dma_start(out=dw_rows[:, m0:m1, h * HALF + n0 : h * HALF + n1], in_=dw_sb[h][:, m0:m1, n0:n1])
+        def store(queue, h, m0, m1, n0, n1):
+            queue.dma_start(out=dw_rows[:, m0:m1, h * HALF + n0 : h * HALF + n1], in_=dw_sb[h][:, m0:m1, n0:n1])
 
         zero_planes(0, 0, 2)
         nc.gpsimd.memset(gain_rows[:], 0.0)
         make_identity(nc, ident[:])
+        zero_planes(0, 2, 4)
+        zero_planes(0, 4, GROUPS)
+        zero_planes(1, 0, GROUPS)
+        load_scales(nc.gpsimd, 0, 4, GROUPS)
+        load_scales(nc.gpsimd, 1, 0, GROUPS)
         nc.gpsimd.memset(early[:], 0.0)
         nc.gpsimd.memset(late[:], 0.0)
-        zero_planes(0, 2, GROUPS)
-        zero_planes(1, 0, GROUPS)
 
         for g in range(GROUPS):
             load_x(g, g + 1)
             if g == 0:
                 nc.sync.dma_start(out=gain_rows[0:M_TILES, :], in_=gain.rearrange("(m d) -> m d", m=M_TILES))
-                load_scales(0, 0, 2)
+                load_scales(nc.sync, 0, 0, 2)
             load_g(0, g, g + 1)
             if g == 1:
-                load_scales(0, 2, GROUPS)
-        load_scales(1, 0, GROUPS)
-        for g in range(GROUPS):
-            load_g(1, g, g + 1)
-            if g == 3:
-                load_w(0, 1)
-        for m in range(1, M_TILES):
-            load_w(m, m + 1)
+                load_scales(nc.sync, 0, 2, 4)
+        load_g(1, 0, 1)
+        load_g(1, 1, 2)
+        load_g(1, 2, 4)
+        load_w(0, 1)
+        load_g(1, 4, 6)
+        load_g(1, 6, 8)
+        load_w(1, 2)
+        load_w(2, 4)
 
         nc.vector.tensor_copy(out=ident_bf[:], in_=ident[:])
 
@@ -182,8 +186,8 @@ def tile_up_projection_gain_grads_e2_kernel(tc, x, g_words, g_scales, gain, w, o
 
         for m in range(M_TILES):
             nc.scalar.activation(out=dw_sb[0][:, m, :], in_=a_raw[:, m, :], func=COPY, scale=gain_col[:, m : m + 1])
-        store(0, 0, 2, 0, HALF)
-        store(0, 2, 4, 0, HALF)
+        store(nc.gpsimd, 0, 0, 2, 0, HALF)
+        store(nc.gpsimd, 0, 2, 4, 0, HALF)
 
         def weigh_sweep1(m):
             junk = junkp.tile([P, HALF], F32, name="junk")
@@ -210,18 +214,18 @@ def tile_up_projection_gain_grads_e2_kernel(tc, x, g_words, g_scales, gain, w, o
             for n in range(2):
                 scale_bank(m, n)
                 weigh_bank(m, n, parts[:, m, 1 + n : 2 + n])
-            store(1, m, m + 1, 0, HALF)
+            store(nc.sync, 1, m, m + 1, 0, HALF)
         m = M_TILES - 1
         scale_bank(m, 0)
         weigh_bank(m, 0, parts[:, m, 1:2])
-        store(1, m, m + 1, 0, N)
+        store(nc.sync, 1, m, m + 1, 0, N)
         nc.vector.tensor_reduce(out=early[:, 0:m], in_=parts[:, 0:m, 0:3], axis=AXIS_X, op=ADD)
         nc.vector.tensor_reduce(out=early[:, m : m + 1], in_=parts[:, m : m + 1, 0:2], axis=AXIS_X, op=ADD)
         dg = bank(0, "dg")
         nc.tensor.matmul(dg[:, 0:P], lhsT=early[:], rhs=ident[:], start=True, stop=False)
         weigh_bank(m, 1, late[:, m : m + 1])
         scale_bank(m, 1)
-        store(1, m, m + 1, N, HALF)
+        store(nc.sync, 1, m, m + 1, N, HALF)
         nc.tensor.matmul(dg[:, 0:P], lhsT=late[:], rhs=ident[:], start=False, stop=True)
         nc.scalar.copy(dgain_sb[:], dg[0:M_TILES, 0:P])
         nc.sync.dma_start(out=out_1.rearrange("(m d) -> m d", m=M_TILES), in_=dgain_sb[:])

from contextlib import ExitStack

import concourse.mybir as mybir
from concourse.masks import make_identity

T, D, F = 4096, 512, 2048
FLOPS = 2 * T * D * F

F32 = mybir.dt.float32
BF16 = mybir.dt.bfloat16
I32 = mybir.dt.int32
U32 = mybir.dt.uint32
U8 = mybir.dt.uint8
E4X4 = mybir.dt.float8_e4m3fn_x4
E5X4 = mybir.dt.float8_e5m2_x4
MULT = mybir.AluOpType.mult
ADD = mybir.AluOpType.add
COPY = mybir.ActivationFunctionType.Copy
AXIS_X = mybir.AxisListType.X

P = 128
PACK = 4
GROUPS = T // (P * PACK)
M_TILES = D // P
N = 512
HALF = 1024
SCALE_BATCHES = ((0, 0, 2), (0, 2, 4), (0, 4, GROUPS), (1, 0, GROUPS))


def tile_up_projection_gain_grads_e2_kernel(tc, x, g_words, g_scales, gain, w, out_0, out_1):
    nc = tc.nc
    x_rows = x.rearrange("(g p j) d -> p g (j d)", p=P, j=PACK)
    words = g_words.rearrange("g p n t -> p g (n t)")
    scale_rows = g_scales.bitcast(I32).rearrange("g (q r) n -> r q g n", r=4)
    w_rows = w.rearrange("(m p) n -> p m n", p=P)
    dw_rows = out_0.rearrange("(m p) n -> p m n", p=P)

    with ExitStack() as ctx:
        keep = ctx.enter_context(tc.tile_pool(name="keep", bufs=1))
        grp = ctx.enter_context(tc.tile_pool(name="grp", bufs=3))
        junkp = ctx.enter_context(tc.tile_pool(name="junkp", bufs=2))
        psum = ctx.enter_context(tc.psum_pool(name="psum", bufs=1))
        ctx.enter_context(tc.manual_schedule())

        x_raw = keep.tile([P, GROUPS, PACK, D], BF16, name="x_raw", align_bytes=64)
        x_codes = keep.tile([P, GROUPS, D], U32, name="x_codes", align_bytes=64)
        x_scales = keep.tile([P, GROUPS, D], U8, name="x_scales", align_bytes=64)
        g_codes = [keep.tile([P, GROUPS, HALF], U32, name=f"g_codes{h}", align_bytes=64) for h in range(2)]
        g_planes = {
            (h, g0, g1): keep.tile([P, g1 - g0, HALF], U8, name=f"g_planes{h}_{g0}", align_bytes=64)
            for h, g0, g1 in SCALE_BATCHES
        }

        def plane(h, g):
            for hh, g0, g1 in SCALE_BATCHES:
                if hh == h and g0 <= g < g1:
                    return g_planes[hh, g0, g1][:, g - g0, :]
            raise ValueError("no scale tile for this group")
        w_sb = keep.tile([P, M_TILES, F], BF16, name="w_sb", align_bytes=64)
        a_raw = keep.tile([P, M_TILES, HALF], F32, name="a_raw", align_bytes=64)
        dw_sb = [keep.tile([P, M_TILES, HALF], F32, name=f"dw_sb{h}", align_bytes=64) for h in range(2)]
        gain_rows = keep.tile([P, P], BF16, name="gain_rows", align_bytes=64)
        gain_col = keep.tile([P, M_TILES], F32, name="gain_col", align_bytes=64)
        ident = keep.tile([P, P], F32, name="ident", align_bytes=64)
        ident_bf = keep.tile([P, P], BF16, name="ident_bf", align_bytes=64)
        early = keep.tile([P, P], F32, name="early", align_bytes=64)
        late = keep.tile([P, P], F32, name="late", align_bytes=64)
        parts = keep.tile([P, M_TILES, 4], F32, name="parts", align_bytes=64)
        dgain_sb = keep.tile([M_TILES, P], F32, name="dgain_sb", align_bytes=64)

        def bank(b, what):
            return psum.tile([P, N], F32, name=what, tag=f"bank{b}")

        def zero_planes(h, g0, g1):
            nc.vector.memset(g_planes[h, g0, g1][:].rearrange("p g n -> p (g n)").bitcast(I32), 0)

        def load_scales(queue, h, g0, g1):
            for r in range(4):
                queue.dma_start(
                    out=g_planes[h, g0, g1][r:P:32].bitcast(I32),
                    in_=scale_rows[r, :, g0:g1, h * (HALF // 4) : (h + 1) * (HALF // 4)],
                )

        def load_x(g0, g1):
            nc.sync.dma_start(out=x_raw[:, g0:g1].rearrange("p g j d -> p g (j d)"), in_=x_rows[:, g0:g1, :])

        def load_g(h, g0, g1):
            nc.sync.dma_start(
                out=g_codes[h][:, g0:g1, :].bitcast(I32),
                in_=words[:, g0:g1, h * HALF * 4 : (h + 1) * HALF * 4].bitcast(I32),
            )

        def load_w(m0, m1):
            nc.sync.dma_start(out=w_sb[:, m0:m1, :], in_=w_rows[:, m0:m1, :])

        def store(queue, h, m0, m1, n0, n1):
            queue.dma_start(out=dw_rows[:, m0:m1, h * HALF + n0 : h * HALF + n1], in_=dw_sb[h][:, m0:m1, n0:n1])

        zero_planes(0, 0, 2)
        nc.gpsimd.memset(gain_rows[:], 0.0)
        make_identity(nc, ident[:])
        zero_planes(0, 2, 4)
        zero_planes(0, 4, GROUPS)
        zero_planes(1, 0, GROUPS)
        load_scales(nc.gpsimd, 0, 4, GROUPS)
        load_scales(nc.gpsimd, 1, 0, GROUPS)
        nc.gpsimd.memset(early[:], 0.0)
        nc.gpsimd.memset(late[:], 0.0)

        for g in range(GROUPS):
            load_x(g, g + 1)
            if g == 0:
                nc.sync.dma_start(out=gain_rows[0:M_TILES, :], in_=gain.rearrange("(m d) -> m d", m=M_TILES))
                load_scales(nc.sync, 0, 0, 2)
            load_g(0, g, g + 1)
            if g == 1:
                load_scales(nc.sync, 0, 2, 4)
        load_g(1, 0, 1)
        load_g(1, 1, 2)
        load_g(1, 2, 4)
        load_w(0, 1)
        load_g(1, 4, 6)
        load_g(1, 6, 8)
        load_w(1, 2)
        load_w(2, 4)

        nc.vector.tensor_copy(out=ident_bf[:], in_=ident[:])

        gain_ps = bank(7, "gain_ps")
        nc.tensor.matmul(gain_ps[:, 0:M_TILES], lhsT=gain_rows[:], rhs=ident_bf[:, 0:M_TILES], start=True, stop=True)

        def quantise(g):
            lay = grp.tile([P, D, PACK], BF16, name="lay", align_bytes=64)
            src = x_raw[:, g].rearrange("p j d -> p d j")
            for a in (0, 128):
                nc.vector.tensor_copy(out=lay[:, a : a + 128, :], in_=src[:, a : a + 128, :])
            for a in (256, 384):
                nc.scalar.copy(lay[:, a : a + 128, :], src[:, a : a + 128, :])
            for a, b in ((0, 128), (128, 256), (256, 512)):
                nc.vector.quantize_mx(
                    out=x_codes[:, g, a:b].bitcast(E4X4),
                    scales=x_scales[:, g, a:b],
                    in_=lay[:, a:b, :].rearrange("p d j -> p (d j)"),
                )

        def mx_pass(acc, h, g, m, n):
            nc.tensor.matmul_mx(
                out=acc[:],
                lhsT=x_codes[:, g, m * P : (m + 1) * P].bitcast(E4X4),
                lhsT_scale=x_scales[:, g, m * P : (m + 1) * P],
                rhs=g_codes[h][:, g, n * N : (n + 1) * N].bitcast(E5X4),
                rhs_scale=plane(h, g)[:, n * N : (n + 1) * N],
                start=(g == 0),
                stop=(g == GROUPS - 1),
            )

        acc = [[bank(4 * n + m, f"acc0_{n}_{m}") for m in range(M_TILES)] for n in range(2)]
        for g in range(GROUPS):
            quantise(g)
            if g == 0:
                nc.vector.tensor_copy(out=gain_col[:], in_=gain_ps[:, 0:M_TILES])
            if g < GROUPS - 1:
                for m in range(M_TILES):
                    for n in range(2):
                        mx_pass(acc[n][m], 0, g, m, n)
        for n in range(2):
            for m in range(M_TILES):
                mx_pass(acc[n][m], 0, GROUPS - 1, m, n)
        for n in range(2):
            for m in range(M_TILES):
                half = a_raw[:, m, n * N : (n + 1) * N]
                if m % 2 == 0:
                    nc.scalar.copy(half, acc[n][m][:])
                else:
                    nc.vector.tensor_copy(out=half, in_=acc[n][m][:])

        acc2 = [[bank(2 * m + n, f"acc1_{n}_{m}") for n in range(2)] for m in range(M_TILES)]
        for g in range(GROUPS // 2):
            for m in range(M_TILES):
                for n in range(2):
                    mx_pass(acc2[m][n], 1, g, m, n)
        for m in range(M_TILES):
            for n in range(2):
                for g in range(GROUPS // 2, GROUPS):
                    mx_pass(acc2[m][n], 1, g, m, n)

        for m in range(M_TILES):
            nc.scalar.activation(out=dw_sb[0][:, m, :], in_=a_raw[:, m, :], func=COPY, scale=gain_col[:, m : m + 1])
        store(nc.gpsimd, 0, 0, 2, 0, HALF)
        store(nc.gpsimd, 0, 2, 4, 0, HALF)

        def weigh_sweep1(m):
            junk = junkp.tile([P, HALF], F32, name="junk")
            nc.vector.scalar_tensor_tensor(
                out=junk[:], in0=a_raw[:, m, :], scalar=1.0, in1=w_sb[:, m, 0:HALF], op0=MULT, op1=MULT,
                accum_out=parts[:, m, 0:1],
            )

        def weigh_bank(m, n, into):
            junk = junkp.tile([P, HALF], F32, name="junk")
            nc.vector.scalar_tensor_tensor(
                out=junk[:, 0:N], in0=acc2[m][n][:], scalar=1.0, in1=w_sb[:, m, HALF + n * N : HALF + (n + 1) * N],
                op0=MULT, op1=MULT, accum_out=into,
            )

        def scale_bank(m, n):
            nc.scalar.activation(
                out=dw_sb[1][:, m, n * N : (n + 1) * N], in_=acc2[m][n][:], func=COPY, scale=gain_col[:, m : m + 1]
            )

        weigh_sweep1(0)
        for m in range(M_TILES - 1):
            weigh_sweep1(m + 1)
            for n in range(2):
                scale_bank(m, n)
                weigh_bank(m, n, parts[:, m, 1 + n : 2 + n])
            store(nc.sync, 1, m, m + 1, 0, HALF)
        m = M_TILES - 1
        scale_bank(m, 0)
        weigh_bank(m, 0, parts[:, m, 1:2])
        store(nc.sync, 1, m, m + 1, 0, N)
        nc.vector.tensor_reduce(out=early[:, 0:m], in_=parts[:, 0:m, 0:3], axis=AXIS_X, op=ADD)
        nc.vector.tensor_reduce(out=early[:, m : m + 1], in_=parts[:, m : m + 1, 0:2], axis=AXIS_X, op=ADD)
        dg = bank(0, "dg")
        nc.tensor.matmul(dg[:, 0:P], lhsT=early[:], rhs=ident[:], start=True, stop=False)
        weigh_bank(m, 1, late[:, m : m + 1])
        scale_bank(m, 1)
        store(nc.sync, 1, m, m + 1, N, HALF)
        nc.tensor.matmul(dg[:, 0:P], lhsT=late[:], rhs=ident[:], start=False, stop=True)
        nc.scalar.copy(dgain_sb[:], dg[0:M_TILES, 0:P])
        nc.sync.dma_start(out=out_1.rearrange("(m d) -> m d", m=M_TILES), in_=dgain_sb[:])
